import numpy as np
import ml_dtypes


def mxq(x, axis, fmt="e4m3"):
    dtype, down = {"e4m3": (ml_dtypes.float8_e4m3fn, 7), "e5m2": (ml_dtypes.float8_e5m2, 14)}[fmt]
    v = np.moveaxis(np.asarray(x, np.float32).astype(ml_dtypes.bfloat16).astype(np.float64), axis, -1)
    blocks = v.reshape(v.shape[:-1] + (-1, 32))
    amax = np.abs(blocks).max(-1, keepdims=True)
    byte = np.maximum(np.where(amax > 0, np.frexp(amax)[1] - 1 + 127, 0) - down, 1)
    scale = np.exp2(byte - 127.0)
    codes = (blocks / scale).astype(np.float32).astype(dtype).astype(np.float64)
    return np.moveaxis((codes * scale).reshape(v.shape), -1, axis)


WIDE = False


def mx_kscale(k):
    if not WIDE:
        return np.ones(k)
    levels = np.array([10, -10, 5, -5, 0])
    if k % 512:
        return np.exp2(np.random.permutation(np.resize(levels, k // 32))).repeat(32)
    a = np.empty((k // 512, 16))
    for p in range(k // 512):
        a[p, :8] = np.random.permutation(np.resize(levels, 8))
        for g in range(8):
            far = levels[np.abs(levels - a[p, g]) >= 10]
            a[p, g + 8] = far[np.random.randint(len(far))]
    return np.exp2(a.ravel()).repeat(32)


BF16 = ml_dtypes.bfloat16


def bf(x):
    return np.asarray(x, np.float32).astype(BF16)


def f64(x):
    return np.asarray(x).astype(np.float64)


E2M1 = np.array([0.0, 0.5, 1.0, 1.5, 2.0, 3.0, 4.0, 6.0, -0.0, -0.5, -1.0, -1.5, -2.0, -3.0, -4.0, -6.0])


def pack_weight(w, fmt):
    k, n = w.shape
    w = f64(bf(w)).reshape(k // 32, 32, n)
    amax = np.abs(w).max(1)
    if fmt == "e4m3":
        byte = np.frexp(amax)[1] - 1 + 127 - 7
    else:
        mant, ex = np.frexp(amax / 6.0)
        byte = np.where(mant > 0.5, ex, ex - 1) + 127
    byte = np.clip(np.where(amax > 0, byte, 1), 1, 254)
    scaled = (w * np.exp2(127.0 - byte)[:, None, :]).reshape(k, n).astype(np.float32)
    by_word = np.ascontiguousarray(scaled.reshape(k // 512, 128, 4, n).transpose(0, 1, 3, 2))
    if fmt == "e4m3":
        words = by_word.astype(ml_dtypes.float8_e4m3fn).view(np.uint8)
    else:
        c = by_word.astype(ml_dtypes.float4_e2m1fn).view(np.uint8) & 0xF
        words = c[..., 0::2] | (c[..., 1::2] << 4)
    return np.ascontiguousarray(words), np.ascontiguousarray(byte.astype(np.uint8).reshape(k // 512, 16, n))


def unpack_weight(words, scales, fmt):
    g, p, n, _ = words.shape
    if fmt == "e4m3":
        vals = np.ascontiguousarray(words).view(ml_dtypes.float8_e4m3fn).astype(np.float64)
    else:
        nib = np.empty((g, p, n, 4), np.uint8)
        nib[..., 0::2] = words & 0xF
        nib[..., 1::2] = words >> 4
        vals = E2M1[nib]
    vals = vals * np.repeat(np.exp2(scales.astype(np.float64) - 127.0), 8, axis=1)[..., None]
    return vals.transpose(0, 1, 3, 2).reshape(g * 512, n)
def pack4(w):
    words, scales = pack_weight(w, "e2m1")
    return words.reshape(words.shape[0], 128, -1), scales


def unpack4(words, scales):
    return unpack_weight(words.reshape(words.shape[0], 128, -1, 2), scales, "e2m1")


M, K, F = 512, 1024, 4096


def setup_inputs():
    s = mx_kscale(K)
    t = mx_kscale(F)
    xt = np.random.standard_normal((K, M)) * s[:, None]
    wu = np.random.standard_normal((K, F)) / np.sqrt(K) / s[:, None] * t
    wd = np.random.standard_normal((F, K)) / np.sqrt(F) / t[:, None]
    x_words, x_scales = pack4(xt)
    up_words, up_scales = pack4(wu)
    down_words, down_scales = pack_weight(wd, "e4m3")
    return {"x_words": x_words, "x_scales": x_scales,
            "up_words": up_words, "up_scales": up_scales,
            "z": bf(np.random.standard_normal((M, F))),
            "down_words": down_words, "down_scales": down_scales,
            "res": bf(np.random.standard_normal((M, K)))}


def reference(x_words, x_scales, up_words, up_scales, z, down_words, down_scales, res):
    xt = unpack4(x_words, x_scales)
    wu = unpack4(up_words, up_scales)
    wd = unpack_weight(down_words, down_scales, "e4m3")
    u = xt.T @ wu
    zf = f64(z)
    h = u * (zf / (1.0 + np.exp(-zf)))
    y = mxq(h, 1, "e4m3") @ wd
    return y + f64(res)

@@ -1,0 +1,271 @@
+from contextlib import ExitStack
+
+import concourse.mybir as mybir
+from concourse.masks import make_identity
+
+M, K, F = 512, 1024, 4096
+FLOPS = 2 * M * K * F * 2
+
+F32 = mybir.dt.float32
+BF16 = mybir.dt.bfloat16
+U32 = mybir.dt.uint32
+I32 = mybir.dt.int32
+U8 = mybir.dt.uint8
+FP4X4 = mybir.dt.float4_e2m1fn_x4
+FP8X4 = mybir.dt.float8_e4m3fn_x4
+SILU = mybir.ActivationFunctionType.Silu
+MULT = mybir.AluOpType.mult
+ADD = mybir.AluOpType.add
+
+P = 128
+PASS = 512
+NG = K // PASS
+STEPS = 8
+PAIRS = F // (2 * PASS)
+
+
+def tile_gated_ffn_down_s4_kernel(
+    tc, x_words, x_scales, up_words, up_scales, z, down_words, down_scales, res, out
+):
+    nc = tc.nc
+
+    x_src = x_words.bitcast(I32).rearrange("g p w -> p g w")
+    up_src = up_words.bitcast(I32).rearrange("g p w -> p g w")
+    xs_src = x_scales.bitcast(I32).rearrange("g (Q r) n -> r Q g n", r=4)
+    us_src = up_scales.bitcast(I32).rearrange("g (Q r) n -> r Q g n", r=4)
+    ds_src = down_scales.bitcast(I32)
+    down_src = down_words.rearrange("g p n t -> g p (n t)").bitcast(I32).rearrange("g p w -> p g w")
+    z_src = z.rearrange("(m p) f -> p m f", p=P)
+    res_src = res.rearrange("(m p) n -> p m n", p=P)
+
+    with ExitStack() as ctx:
+        keep = ctx.enter_context(tc.tile_pool(name="keep", bufs=1))
+        work = ctx.enter_context(tc.tile_pool(name="work", bufs=3))
+        psum = ctx.enter_context(tc.psum_pool(name="psum", bufs=1))
+        ctx.enter_context(tc.manual_schedule())
+
+        def keep_tile(name, shape, dtype):
+            return keep.tile(shape, dtype, name=name, align_bytes=64)
+
+        x_sb = keep_tile("x_sb", [P, NG, 2 * M], U8)
+        xs_sb = keep_tile("xs_sb", [P, NG, M], U8)
+        up_sb = [keep_tile("up_sb%d" % j, [P, NG, 2048], U8) for j in range(PAIRS)]
+        us_first = keep_tile("us_first", [P, NG, 1024], U8)
+        us_rest = keep_tile("us_rest", [P, NG, 3072], U8)
+        z_sb = [keep_tile("z_sb%d" % i, [P, 2, 1024], BF16) for i in range(STEPS)]
+        down_sb = [keep_tile("down_sb%d" % j, [P, 2, 1024], U32) for j in range(PAIRS)]
+        ds_sb = [keep_tile("ds_sb%d" % a, [P, 1024], U8) for a in range(2)]
+        res_sb = [keep_tile("res_sb%d" % h, [P, 2, K], BF16) for h in range(2)]
+        ident = keep_tile("ident", [P, P], F32)
+        warm = keep_tile("warm", [P, 1], F32)
+        warm_out = keep_tile("warm_out", [P, 1], F32)
+
+        nc.gpsimd.dma_start(out=x_sb[:].bitcast(I32), in_=x_src)
+        nc.gpsimd.dma_start(out=up_sb[0][:].bitcast(I32)[:, :, 0:256], in_=up_src[:, :, 0:256])
+        make_identity(nc, ident[:])
+
+        nc.vector.memset(xs_sb[:].bitcast(I32), 0)
+        nc.vector.memset(us_first[:].bitcast(I32), 0)
+        nc.vector.memset(warm[:], 0.0)
+        nc.vector.memset(us_rest[:].bitcast(I32), 0)
+        for a in range(2):
+            nc.vector.memset(ds_sb[a][:].bitcast(I32), 0)
+        nc.scalar.activation(out=warm_out[:], in_=warm[:], func=SILU)
+
+        for r in range(4):
+            nc.sync.dma_start(out=xs_sb[:].bitcast(I32)[r:P:32, :, :], in_=xs_src[r])
+        for r in range(4):
+            nc.sync.dma_start(out=us_first[:].bitcast(I32)[r:P:32, :, :], in_=us_src[r][:, :, 0:256])
+
+        def load_up(j):
+            nc.sync.dma_start(out=up_sb[j][:].bitcast(I32), in_=up_src[:, :, 512 * j : 512 * (j + 1)])
+
+        def load_z(i):
+            h, j = divmod(i, PAIRS)
+            nc.sync.dma_start(out=z_sb[i][:], in_=z_src[:, 2 * h : 2 * h + 2, 1024 * j : 1024 * (j + 1)])
+
+        def load_down(j):
+            nc.sync.dma_start(out=down_sb[j][:].bitcast(I32), in_=down_src[:, 2 * j : 2 * j + 2, :])
+
+        def load_res(h):
+            nc.sync.dma_start(out=res_sb[h][:], in_=res_src[:, 2 * h : 2 * h + 2, :])
+
+        nc.sync.dma_start(out=z_sb[0][:, :, 0:512], in_=z_src[:, 0:2, 0:512])
+        nc.sync.dma_start(out=up_sb[0][:].bitcast(I32)[:, :, 256:512], in_=up_src[:, :, 256:512])
+        nc.sync.dma_start(out=z_sb[0][:, :, 512:1024], in_=z_src[:, 0:2, 512:1024])
+        for r in range(4):
+            nc.sync.dma_start(out=us_rest[:].bitcast(I32)[r:P:32, :, :], in_=us_src[r][:, :, 256:1024])
+        load_up(1)
+        load_z(1)
+        for a in range(2):
+            for q in range(4):
+                nc.sync.dma_start(
+                    out=ds_sb[a][:].bitcast(I32)[32 * q : 32 * q + 16, :],
+                    in_=ds_src[4 * a : 4 * a + 4, 4 * q : 4 * q + 4, :],
+                )
+        load_down(0)
+        load_up(2)
+        load_z(2)
+        load_down(1)
+        load_up(3)
+        load_z(3)
+        load_res(0)
+        load_down(2)
+        load_z(4)
+        load_down(3)
+        load_z(5)
+        load_res(1)
+        load_z(6)
+        load_z(7)
+
+        silu_t = {}
+        u_ps = {}
+        h_sb = {}
+        t_ps = {}
+        grouped = {}
+        codes = {}
+        scales = {}
+        y_ps = {}
+
+        def silu(i, k):
+            c, m = divmod(k, 2)
+            s = work.tile([P, PASS], F32, name="s", tag="s", bufs=8)
+            nc.scalar.activation(
+                out=s[:].rearrange("p (u w e) -> p u w e", u=2, e=2),
+                in_=z_sb[i][:, m, PASS * c : PASS * (c + 1)].rearrange("p (w u e) -> p u w e", u=2, e=2),
+                func=SILU,
+            )
+            silu_t[i, k] = s
+
+        def first_product(i, k):
+            h, j = divmod(i, PAIRS)
+            c, m = divmod(k, 2)
+            mt = 2 * h + m
+            u = psum.tile([P, PASS], F32, name="u", tag="u", bufs=2)
+            for g in range(NG):
+                if j == 0:
+                    us = us_first[:, g, PASS * c : PASS * (c + 1)]
+                else:
+                    c0 = 1024 * (j - 1) + PASS * c
+                    us = us_rest[:, g, c0 : c0 + PASS]
+                nc.tensor.matmul_mx(
+                    out=u[:],
+                    lhsT=x_sb[:, g, 256 * mt : 256 * (mt + 1)].bitcast(FP4X4),
+                    lhsT_scale=xs_sb[:, g, P * mt : P * (mt + 1)],
+                    rhs=up_sb[j][:, g, 1024 * c : 1024 * (c + 1)].bitcast(FP4X4),
+                    rhs_scale=us,
+                    start=(g == 0),
+                    stop=(g == NG - 1),
+                )
+            u_ps[i, k] = u
+
+        def gate(i, k):
+            hb = work.tile([P, PASS], BF16, name="hb", tag="hb", bufs=10, align_bytes=64)
+            nc.vector.tensor_tensor(
+                out=hb[:].rearrange("p (u w e) -> p u w e", u=2, e=2),
+                in0=u_ps[i, k][:].rearrange("p (w u e) -> p u w e", u=2, e=2),
+                in1=silu_t[i, k][:].rearrange("p (u w e) -> p u w e", u=2, e=2),
+                op=MULT,
+            )
+            h_sb[i, k] = hb
+
+        def transposes(i, c):
+            t = psum.tile([P, 4, P], F32, name="t", tag="t", bufs=2)
+            for m in range(2):
+                words = h_sb[i, 2 * c + m][:].bitcast(F32)
+                for u in range(2):
+                    nc.tensor.transpose(t[:, 2 * m + u, :], words[:, P * u : P * (u + 1)], ident[:])
+            t_ps[i, c] = t
+
+        def copy_out(i, c, on_vector):
+            if c == 0:
+                grouped[i] = work.tile([P, 2, 1024], BF16, name="gr", tag="gr", bufs=2, align_bytes=64)
+            dst = grouped[i][:, c, :].bitcast(F32).rearrange("p (m n u) -> p m n u", m=2, u=2)
+            srcv = t_ps[i, c][:].rearrange("p (m u) n -> p m n u", u=2)
+            if on_vector:
+                nc.vector.tensor_copy(out=dst, in_=srcv)
+            else:
+                nc.scalar.copy(out=dst, in_=srcv)
+
+        def new_codes(i):
+            codes[i] = work.tile([P, 2, 256], U32, name="cd", tag="cd", bufs=3, align_bytes=64)
+            scales[i] = work.tile([P, 2, 256], U8, name="sc", tag="sc", bufs=3, align_bytes=64)
+
+        def quantise(i):
+            new_codes(i)
+            nc.vector.quantize_mx(
+                out=codes[i][:].rearrange("p c n -> p (c n)").bitcast(FP8X4),
+                scales=scales[i][:].rearrange("p c n -> p (c n)"),
+                in_=grouped[i][:].rearrange("p c n -> p (c n)"),
+            )
+
+        def quantise_half(i, c):
+            if c == 0:
+                new_codes(i)
+            nc.vector.quantize_mx(
+                out=codes[i][:, c, :].bitcast(FP8X4),
+                scales=scales[i][:, c, :],
+                in_=grouped[i][:, c, :],
+            )
+
+        def second_product(i, a):
+            j = i % PAIRS
+            m, nh = divmod(a, 2)
+            if j == 0:
+                y_ps[a] = psum.tile([P, 512], F32, name="y%d" % a, tag="y%d" % a, bufs=1)
+            for c in range(2):
+                g = 2 * j + c
+                nc.tensor.matmul_mx(
+                    out=y_ps[a][:],
+                    lhsT=codes[i][:, c, P * m : P * (m + 1)].bitcast(FP8X4),
+                    lhsT_scale=scales[i][:, c, P * m : P * (m + 1)],
+                    rhs=down_sb[j][:, c, 512 * nh : 512 * (nh + 1)].bitcast(FP8X4),
+                    rhs_scale=ds_sb[g // 4][4 * (g % 4) : P, 512 * nh : 512 * (nh + 1)],
+                    start=(g == 0),
+                    stop=(g == 2 * PAIRS - 1),
+                )
+
+        def finish(h, a):
+            m, nh = divmod(a, 2)
+            mt = 2 * h + m
+            o = work.tile([P, 512], F32, name="o", tag="o", bufs=8)
+            cols = slice(512 * nh, 512 * (nh + 1))
+            nc.vector.tensor_tensor(out=o[:], in0=y_ps[a][:], in1=res_sb[h][:, m, cols], op=ADD)
+            nc.sync.dma_start(out=out[P * mt : P * (mt + 1), cols], in_=o[:])
+
+        for k in range(4):
+            silu(0, k)
+        for i in range(STEPS):
+            for k in range(4):
+                first_product(i, k)
+                if i >= 2:
+                    second_product(i - 2, k)
+                gate(i, k)
+                if i == 5 and k >= 2:
+                    finish(0, k - 2)
+                if i == 6 and k < 2:
+                    finish(0, k + 2)
+                if k == 0:
+                    if i >= 1:
+                        transposes(i - 1, 0)
+                        transposes(i - 1, 1)
+                        copy_out(i - 1, 0, False)
+                        copy_out(i - 1, 1, False)
+                    if i + 1 < STEPS:
+                        for kk in range(4):
+                            silu(i + 1, kk)
+                if k == 1 and i >= 1:
+                    quantise(i - 1)
+        last = STEPS - 1
+        second_product(last - 1, 0)
+        transposes(last, 0)
+        copy_out(last, 0, False)
+        transposes(last, 1)
+        copy_out(last, 1, True)
+        quantise_half(last, 0)
+        quantise_half(last, 1)
+        for k in range(1, 4):
+            second_product(last - 1, k)
+        for k in range(4):
+            second_product(last, k)
+            finish(1, k)

@@ -21,6 +21,7 @@ P = 128
 PASS = 512
 NG = K // PASS
 STEPS = 8
+LAG = 4
 PAIRS = F // (2 * PASS)
 
 
@@ -60,8 +61,9 @@ def tile_gated_ffn_down_s4_kernel(
         warm = keep_tile("warm", [P, 1], F32)
         warm_out = keep_tile("warm_out", [P, 1], F32)
 
-        nc.gpsimd.dma_start(out=x_sb[:].bitcast(I32), in_=x_src)
-        nc.gpsimd.dma_start(out=up_sb[0][:].bitcast(I32)[:, :, 0:256], in_=up_src[:, :, 0:256])
+        nc.gpsimd.dma_start(out=z_sb[0][:, :, 0:512], in_=z_src[:, 0:2, 0:512])
+        nc.sync.dma_start(out=x_sb[:].bitcast(I32), in_=x_src)
+        nc.sync.dma_start(out=up_sb[0][:].bitcast(I32)[:, :, 0:256], in_=up_src[:, :, 0:256])
         make_identity(nc, ident[:])
 
         nc.vector.memset(xs_sb[:].bitcast(I32), 0)
@@ -90,33 +92,32 @@ def tile_gated_ffn_down_s4_kernel(
         def load_res(h):
             nc.sync.dma_start(out=res_sb[h][:], in_=res_src[:, 2 * h : 2 * h + 2, :])
 
-        nc.sync.dma_start(out=z_sb[0][:, :, 0:512], in_=z_src[:, 0:2, 0:512])
         nc.sync.dma_start(out=up_sb[0][:].bitcast(I32)[:, :, 256:512], in_=up_src[:, :, 256:512])
         nc.sync.dma_start(out=z_sb[0][:, :, 512:1024], in_=z_src[:, 0:2, 512:1024])
         for r in range(4):
             nc.sync.dma_start(out=us_rest[:].bitcast(I32)[r:P:32, :, :], in_=us_src[r][:, :, 256:1024])
         load_up(1)
         load_z(1)
+        load_up(2)
+        load_z(2)
         for a in range(2):
             for q in range(4):
                 nc.sync.dma_start(
                     out=ds_sb[a][:].bitcast(I32)[32 * q : 32 * q + 16, :],
                     in_=ds_src[4 * a : 4 * a + 4, 4 * q : 4 * q + 4, :],
                 )
-        load_down(0)
-        load_up(2)
-        load_z(2)
-        load_down(1)
         load_up(3)
         load_z(3)
-        load_res(0)
-        load_down(2)
+        load_down(0)
         load_z(4)
-        load_down(3)
+        load_down(1)
         load_z(5)
-        load_res(1)
+        load_down(2)
         load_z(6)
+        load_res(0)
+        load_down(3)
         load_z(7)
+        load_res(1)
 
         silu_t = {}
         u_ps = {}
@@ -141,7 +142,8 @@ def tile_gated_ffn_down_s4_kernel(
             h, j = divmod(i, PAIRS)
             c, m = divmod(k, 2)
             mt = 2 * h + m
-            u = psum.tile([P, PASS], F32, name="u", tag="u", bufs=2)
+            bank = ("u0", "u1", "y0", "y1")[k] if i < PAIRS else ("u0", "u1")[k % 2]
+            u = psum.tile([P, PASS], F32, name=bank, tag=bank)
             for g in range(NG):
                 if j == 0:
                     us = us_first[:, g, PASS * c : PASS * (c + 1)]
@@ -170,7 +172,8 @@ def tile_gated_ffn_down_s4_kernel(
             h_sb[i, k] = hb
 
         def transposes(i, c):
-            t = psum.tile([P, 4, P], F32, name="t", tag="t", bufs=2)
+            bank = ("y2", "y3")[c] if i in (0, 2) else ("t0", "t1")[c]
+            t = psum.tile([P, 4, P], F32, name=bank, tag=bank)
             for m in range(2):
                 words = h_sb[i, 2 * c + m][:].bitcast(F32)
                 for u in range(2):
@@ -188,8 +191,8 @@ def tile_gated_ffn_down_s4_kernel(
                 nc.scalar.copy(out=dst, in_=srcv)
 
         def new_codes(i):
-            codes[i] = work.tile([P, 2, 256], U32, name="cd", tag="cd", bufs=3, align_bytes=64)
-            scales[i] = work.tile([P, 2, 256], U8, name="sc", tag="sc", bufs=3, align_bytes=64)
+            codes[i] = work.tile([P, 2, 256], U32, name="cd", tag="cd", bufs=STEPS, align_bytes=64)
+            scales[i] = work.tile([P, 2, 256], U8, name="sc", tag="sc", bufs=STEPS, align_bytes=64)
 
         def quantise(i):
             new_codes(i)
@@ -199,73 +202,73 @@ def tile_gated_ffn_down_s4_kernel(
                 in_=grouped[i][:].rearrange("p c n -> p (c n)"),
             )
 
-        def quantise_half(i, c):
-            if c == 0:
-                new_codes(i)
-            nc.vector.quantize_mx(
-                out=codes[i][:, c, :].bitcast(FP8X4),
-                scales=scales[i][:, c, :],
-                in_=grouped[i][:, c, :],
-            )
-
-        def second_product(i, a):
-            j = i % PAIRS
+        def second_product(i, a, bank, col, width):
+            h, j = divmod(i, PAIRS)
             m, nh = divmod(a, 2)
             if j == 0:
-                y_ps[a] = psum.tile([P, 512], F32, name="y%d" % a, tag="y%d" % a, bufs=1)
+                y_ps[h, a, col] = psum.tile([P, width], F32, name=bank, tag=bank)
+            first = 512 * nh + col
             for c in range(2):
                 g = 2 * j + c
                 nc.tensor.matmul_mx(
-                    out=y_ps[a][:],
+                    out=y_ps[h, a, col][:],
                     lhsT=codes[i][:, c, P * m : P * (m + 1)].bitcast(FP8X4),
                     lhsT_scale=scales[i][:, c, P * m : P * (m + 1)],
-                    rhs=down_sb[j][:, c, 512 * nh : 512 * (nh + 1)].bitcast(FP8X4),
-                    rhs_scale=ds_sb[g // 4][4 * (g % 4) : P, 512 * nh : 512 * (nh + 1)],
+                    rhs=down_sb[j][:, c, first : first + width].bitcast(FP8X4),
+                    rhs_scale=ds_sb[g // 4][4 * (g % 4) : P, first : first + width],
                     start=(g == 0),
                     stop=(g == 2 * PAIRS - 1),
                 )
 
-        def finish(h, a):
+        def finish(h, a, col, width):
             m, nh = divmod(a, 2)
             mt = 2 * h + m
             o = work.tile([P, 512], F32, name="o", tag="o", bufs=8)
-            cols = slice(512 * nh, 512 * (nh + 1))
-            nc.vector.tensor_tensor(out=o[:], in0=y_ps[a][:], in1=res_sb[h][:, m, cols], op=ADD)
-            nc.sync.dma_start(out=out[P * mt : P * (mt + 1), cols], in_=o[:])
+            cols = slice(512 * nh + col, 512 * nh + col + width)
+            nc.vector.tensor_tensor(out=o[:, 0:width], in0=y_ps[h, a, col][:], in1=res_sb[h][:, m, cols], op=ADD)
+            nc.sync.dma_start(out=out[P * mt : P * (mt + 1), cols], in_=o[:, 0:width])
 
         for k in range(4):
             silu(0, k)
         for i in range(STEPS):
             for k in range(4):
                 first_product(i, k)
-                if i >= 2:
-                    second_product(i - 2, k)
+                if i >= LAG:
+                    second_product(i - LAG, k, "y%d" % k, 0, 512)
                 gate(i, k)
-                if i == 5 and k >= 2:
-                    finish(0, k - 2)
-                if i == 6 and k < 2:
-                    finish(0, k + 2)
+                if i == STEPS - 1 and k >= 2:
+                    finish(0, k - 2, 0, 512)
                 if k == 0:
                     if i >= 1:
                         transposes(i - 1, 0)
                         transposes(i - 1, 1)
                         copy_out(i - 1, 0, False)
-                        copy_out(i - 1, 1, False)
+                        copy_out(i - 1, 1, i - 1 in (0, 2))
                     if i + 1 < STEPS:
                         for kk in range(4):
                             silu(i + 1, kk)
                 if k == 1 and i >= 1:
                     quantise(i - 1)
         last = STEPS - 1
-        second_product(last - 1, 0)
+        second_product(4, 0, "y0", 0, 512)
+        second_product(5, 0, "y0", 0, 512)
         transposes(last, 0)
         copy_out(last, 0, False)
         transposes(last, 1)
         copy_out(last, 1, True)
-        quantise_half(last, 0)
-        quantise_half(last, 1)
-        for k in range(1, 4):
-            second_product(last - 1, k)
-        for k in range(4):
-            second_product(last, k)
-            finish(1, k)
+        finish(0, 2, 0, 512)
+        quantise(last)
+        finish(0, 3, 0, 512)
+        second_product(6, 0, "y0", 0, 512)
+        for i in range(4, 7):
+            second_product(i, 1, "y1", 0, 512)
+        for a in range(2):
+            second_product(last, a, "y%d" % a, 0, 512)
+            finish(1, a, 0, 512)
+        for i in range(4, 8):
+            second_product(i, 2, "y2", 0, 512)
+        finish(1, 2, 0, 512)
+        for col in (0, 256):
+            for i in range(4, 8):
+                second_product(i, 3, "u%d" % (col // 256), col, 256)
+            finish(1, 3, col, 256)

@@ -21,7 +21,8 @@ P = 128
 PASS = 512
 NG = K // PASS
 STEPS = 8
-LAG = 4
+LAG = 2
+ORDER = (0, 2, 1, 3)
 PAIRS = F // (2 * PASS)
 
 
@@ -52,7 +53,8 @@ def tile_gated_ffn_down_s4_kernel(
         xs_sb = keep_tile("xs_sb", [P, NG, M], U8)
         up_sb = [keep_tile("up_sb%d" % j, [P, NG, 2048], U8) for j in range(PAIRS)]
         us_first = keep_tile("us_first", [P, NG, 1024], U8)
-        us_rest = keep_tile("us_rest", [P, NG, 3072], U8)
+        us_second = keep_tile("us_second", [P, NG, 1024], U8)
+        us_rest = keep_tile("us_rest", [P, NG, 2048], U8)
         z_sb = [keep_tile("z_sb%d" % i, [P, 2, 1024], BF16) for i in range(STEPS)]
         down_sb = [keep_tile("down_sb%d" % j, [P, 2, 1024], U32) for j in range(PAIRS)]
         ds_sb = [keep_tile("ds_sb%d" % a, [P, 1024], U8) for a in range(2)]
@@ -61,62 +63,71 @@ def tile_gated_ffn_down_s4_kernel(
         warm = keep_tile("warm", [P, 1], F32)
         warm_out = keep_tile("warm_out", [P, 1], F32)
 
-        nc.gpsimd.dma_start(out=z_sb[0][:, :, 0:512], in_=z_src[:, 0:2, 0:512])
-        nc.sync.dma_start(out=x_sb[:].bitcast(I32), in_=x_src)
-        nc.sync.dma_start(out=up_sb[0][:].bitcast(I32)[:, :, 0:256], in_=up_src[:, :, 0:256])
-        make_identity(nc, ident[:])
+        def load_us(plane, first, end):
+            for r in range(4):
+                nc.sync.dma_start(out=plane[:].bitcast(I32)[r:P:32, :, :], in_=us_src[r][:, :, first:end])
 
+        def load_ds(a):
+            for q in range(4):
+                nc.sync.dma_start(
+                    out=ds_sb[a][:].bitcast(I32)[32 * q : 32 * q + 16, :],
+                    in_=ds_src[4 * a : 4 * a + 4, 4 * q : 4 * q + 4, :],
+                )
+
+        nc.gpsimd.dma_start(out=x_sb[:].bitcast(I32), in_=x_src)
+        nc.gpsimd.dma_start(out=z_sb[0][:, :, 0:512], in_=z_src[:, 0:2, 0:512])
+        nc.sync.dma_start(out=up_sb[0][:].bitcast(I32)[:, :, 0:256], in_=up_src[:, :, 0:256])
         nc.vector.memset(xs_sb[:].bitcast(I32), 0)
         nc.vector.memset(us_first[:].bitcast(I32), 0)
         nc.vector.memset(warm[:], 0.0)
+        nc.vector.memset(us_second[:].bitcast(I32), 0)
+        nc.vector.memset(ds_sb[0][:].bitcast(I32), 0)
         nc.vector.memset(us_rest[:].bitcast(I32), 0)
-        for a in range(2):
-            nc.vector.memset(ds_sb[a][:].bitcast(I32), 0)
+        nc.vector.memset(ds_sb[1][:].bitcast(I32), 0)
         nc.scalar.activation(out=warm_out[:], in_=warm[:], func=SILU)
 
         for r in range(4):
             nc.sync.dma_start(out=xs_sb[:].bitcast(I32)[r:P:32, :, :], in_=xs_src[r])
-        for r in range(4):
-            nc.sync.dma_start(out=us_first[:].bitcast(I32)[r:P:32, :, :], in_=us_src[r][:, :, 0:256])
+        load_us(us_first, 0, 256)
+        make_identity(nc, ident[:])
 
         def load_up(j):
             nc.sync.dma_start(out=up_sb[j][:].bitcast(I32), in_=up_src[:, :, 512 * j : 512 * (j + 1)])
 
         def load_z(i):
-            h, j = divmod(i, PAIRS)
+            j, h = divmod(i, 2)
             nc.sync.dma_start(out=z_sb[i][:], in_=z_src[:, 2 * h : 2 * h + 2, 1024 * j : 1024 * (j + 1)])
 
-        def load_down(j):
-            nc.sync.dma_start(out=down_sb[j][:].bitcast(I32), in_=down_src[:, 2 * j : 2 * j + 2, :])
+        def load_down(j, first, end):
+            nc.sync.dma_start(
+                out=down_sb[j][:].bitcast(I32)[:, :, first:end], in_=down_src[:, 2 * j : 2 * j + 2, first:end]
+            )
 
         def load_res(h):
             nc.sync.dma_start(out=res_sb[h][:], in_=res_src[:, 2 * h : 2 * h + 2, :])
 
         nc.sync.dma_start(out=up_sb[0][:].bitcast(I32)[:, :, 256:512], in_=up_src[:, :, 256:512])
         nc.sync.dma_start(out=z_sb[0][:, :, 512:1024], in_=z_src[:, 0:2, 512:1024])
-        for r in range(4):
-            nc.sync.dma_start(out=us_rest[:].bitcast(I32)[r:P:32, :, :], in_=us_src[r][:, :, 256:1024])
-        load_up(1)
         load_z(1)
-        load_up(2)
+        load_us(us_second, 256, 512)
+        load_up(1)
         load_z(2)
-        for a in range(2):
-            for q in range(4):
-                nc.sync.dma_start(
-                    out=ds_sb[a][:].bitcast(I32)[32 * q : 32 * q + 16, :],
-                    in_=ds_src[4 * a : 4 * a + 4, 4 * q : 4 * q + 4, :],
-                )
-        load_up(3)
+        load_ds(0)
+        load_down(0, 0, 512)
         load_z(3)
-        load_down(0)
+        load_down(0, 512, 1024)
+        load_us(us_rest, 512, 1024)
+        load_up(2)
         load_z(4)
-        load_down(1)
         load_z(5)
-        load_down(2)
+        load_down(1, 0, 1024)
+        load_up(3)
         load_z(6)
-        load_res(0)
-        load_down(3)
+        load_ds(1)
         load_z(7)
+        load_down(2, 0, 1024)
+        load_res(0)
+        load_down(3, 0, 1024)
         load_res(1)
 
         silu_t = {}
@@ -139,16 +150,18 @@ def tile_gated_ffn_down_s4_kernel(
             silu_t[i, k] = s
 
         def first_product(i, k):
-            h, j = divmod(i, PAIRS)
+            j, h = divmod(i, 2)
             c, m = divmod(k, 2)
             mt = 2 * h + m
-            bank = ("u0", "u1", "y0", "y1")[k] if i < PAIRS else ("u0", "u1")[k % 2]
+            bank = ("u0", "u1", "y0", "y1")[k] if i < LAG else ("u0", "u1")[k % 2]
             u = psum.tile([P, PASS], F32, name=bank, tag=bank)
             for g in range(NG):
                 if j == 0:
                     us = us_first[:, g, PASS * c : PASS * (c + 1)]
+                elif j == 1:
+                    us = us_second[:, g, PASS * c : PASS * (c + 1)]
                 else:
-                    c0 = 1024 * (j - 1) + PASS * c
+                    c0 = 1024 * (j - 2) + PASS * c
                     us = us_rest[:, g, c0 : c0 + PASS]
                 nc.tensor.matmul_mx(
                     out=u[:],
@@ -172,7 +185,7 @@ def tile_gated_ffn_down_s4_kernel(
             h_sb[i, k] = hb
 
         def transposes(i, c):
-            bank = ("y2", "y3")[c] if i in (0, 2) else ("t0", "t1")[c]
+            bank = ("y2", "y3")[c] if i == 0 else ("t0", "t1")[c]
             t = psum.tile([P, 4, P], F32, name=bank, tag=bank)
             for m in range(2):
                 words = h_sb[i, 2 * c + m][:].bitcast(F32)
@@ -203,7 +216,7 @@ def tile_gated_ffn_down_s4_kernel(
             )
 
         def second_product(i, a, bank, col, width):
-            h, j = divmod(i, PAIRS)
+            j, h = divmod(i, 2)
             m, nh = divmod(a, 2)
             if j == 0:
                 y_ps[h, a, col] = psum.tile([P, width], F32, name=bank, tag=bank)
@@ -233,11 +246,10 @@ def tile_gated_ffn_down_s4_kernel(
         for i in range(STEPS):
             for k in range(4):
                 first_product(i, k)
-                if i >= LAG:
-                    second_product(i - LAG, k, "y%d" % k, 0, 512)
+                if i >= LAG and k % 2 == 1:
+                    j, n = divmod(2 * (i - LAG) + k // 2, 4)
+                    second_product(2 * j, ORDER[n], "y%d" % n, 0, 512)
                 gate(i, k)
-                if i == STEPS - 1 and k >= 2:
-                    finish(0, k - 2, 0, 512)
                 if k == 0:
                     if i >= 1:
                         transposes(i - 1, 0)
@@ -250,25 +262,18 @@ def tile_gated_ffn_down_s4_kernel(
                 if k == 1 and i >= 1:
                     quantise(i - 1)
         last = STEPS - 1
-        second_product(4, 0, "y0", 0, 512)
-        second_product(5, 0, "y0", 0, 512)
-        transposes(last, 0)
-        copy_out(last, 0, False)
-        transposes(last, 1)
-        copy_out(last, 1, True)
-        finish(0, 2, 0, 512)
-        quantise(last)
-        finish(0, 3, 0, 512)
-        second_product(6, 0, "y0", 0, 512)
-        for i in range(4, 7):
-            second_product(i, 1, "y1", 0, 512)
-        for a in range(2):
-            second_product(last, a, "y%d" % a, 0, 512)
-            finish(1, a, 0, 512)
-        for i in range(4, 8):
-            second_product(i, 2, "y2", 0, 512)
-        finish(1, 2, 0, 512)
-        for col in (0, 256):
-            for i in range(4, 8):
-                second_product(i, 3, "u%d" % (col // 256), col, 256)
-            finish(1, 3, col, 256)
+        for n in range(4):
+            second_product(6, ORDER[n], "y%d" % n, 0, 512)
+            finish(0, ORDER[n], 0, 512)
+            if n == 0:
+                transposes(last, 0)
+                copy_out(last, 0, False)
+                transposes(last, 1)
+                copy_out(last, 1, True)
+            if n == 1:
+                quantise(last)
+        for a in range(4):
+            for col in (0,) if a < 3 else (0, 256):
+                for i in range(1, STEPS, 2):
+                    second_product(i, a, ("u0", "u1", "t0", "t1", "y0")[a + col // 256], col, 512 if a < 3 else 256)
+                finish(1, a, col, 512 if a < 3 else 256)

from contextlib import ExitStack

import concourse.mybir as mybir
from concourse.masks import make_identity

M, K, F = 512, 1024, 4096
FLOPS = 2 * M * K * F * 2

F32 = mybir.dt.float32
BF16 = mybir.dt.bfloat16
U32 = mybir.dt.uint32
I32 = mybir.dt.int32
U8 = mybir.dt.uint8
FP4X4 = mybir.dt.float4_e2m1fn_x4
FP8X4 = mybir.dt.float8_e4m3fn_x4
SILU = mybir.ActivationFunctionType.Silu
MULT = mybir.AluOpType.mult
ADD = mybir.AluOpType.add

P = 128
PASS = 512
NG = K // PASS
STEPS = 8
LAG = 2
ORDER = (0, 2, 1, 3)
PAIRS = F // (2 * PASS)


def tile_gated_ffn_down_s4_kernel(
    tc, x_words, x_scales, up_words, up_scales, z, down_words, down_scales, res, out
):
    nc = tc.nc

    x_src = x_words.bitcast(I32).rearrange("g p w -> p g w")
    up_src = up_words.bitcast(I32).rearrange("g p w -> p g w")
    xs_src = x_scales.bitcast(I32).rearrange("g (Q r) n -> r Q g n", r=4)
    us_src = up_scales.bitcast(I32).rearrange("g (Q r) n -> r Q g n", r=4)
    ds_src = down_scales.bitcast(I32)
    down_src = down_words.rearrange("g p n t -> g p (n t)").bitcast(I32).rearrange("g p w -> p g w")
    z_src = z.rearrange("(m p) f -> p m f", p=P)
    res_src = res.rearrange("(m p) n -> p m n", p=P)

    with ExitStack() as ctx:
        keep = ctx.enter_context(tc.tile_pool(name="keep", bufs=1))
        work = ctx.enter_context(tc.tile_pool(name="work", bufs=3))
        psum = ctx.enter_context(tc.psum_pool(name="psum", bufs=1))
        ctx.enter_context(tc.manual_schedule())

        def keep_tile(name, shape, dtype):
            return keep.tile(shape, dtype, name=name, align_bytes=64)

        x_sb = keep_tile("x_sb", [P, NG, 2 * M], U8)
        xs_sb = keep_tile("xs_sb", [P, NG, M], U8)
        up_sb = [keep_tile("up_sb%d" % j, [P, NG, 2048], U8) for j in range(PAIRS)]
        us_first = keep_tile("us_first", [P, NG, 1024], U8)
        us_second = keep_tile("us_second", [P, NG, 1024], U8)
        us_rest = keep_tile("us_rest", [P, NG, 2048], U8)
        z_sb = [keep_tile("z_sb%d" % i, [P, 2, 1024], BF16) for i in range(STEPS)]
        down_sb = [keep_tile("down_sb%d" % j, [P, 2, 1024], U32) for j in range(PAIRS)]
        ds_sb = [keep_tile("ds_sb%d" % a, [P, 1024], U8) for a in range(2)]
        res_sb = [keep_tile("res_sb%d" % h, [P, 2, K], BF16) for h in range(2)]
        ident = keep_tile("ident", [P, P], F32)
        warm = keep_tile("warm", [P, 1], F32)
        warm_out = keep_tile("warm_out", [P, 1], F32)

        def load_us(plane, first, end):
            for r in range(4):
                nc.sync.dma_start(out=plane[:].bitcast(I32)[r:P:32, :, :], in_=us_src[r][:, :, first:end])

        def load_ds(a):
            for q in range(4):
                nc.sync.dma_start(
                    out=ds_sb[a][:].bitcast(I32)[32 * q : 32 * q + 16, :],
                    in_=ds_src[4 * a : 4 * a + 4, 4 * q : 4 * q + 4, :],
                )

        nc.gpsimd.dma_start(out=x_sb[:].bitcast(I32), in_=x_src)
        nc.gpsimd.dma_start(out=z_sb[0][:, :, 0:512], in_=z_src[:, 0:2, 0:512])
        nc.sync.dma_start(out=up_sb[0][:].bitcast(I32)[:, :, 0:256], in_=up_src[:, :, 0:256])
        nc.vector.memset(xs_sb[:].bitcast(I32), 0)
        nc.vector.memset(us_first[:].bitcast(I32), 0)
        nc.vector.memset(warm[:], 0.0)
        nc.vector.memset(us_second[:].bitcast(I32), 0)
        nc.vector.memset(ds_sb[0][:].bitcast(I32), 0)
        nc.vector.memset(us_rest[:].bitcast(I32), 0)
        nc.vector.memset(ds_sb[1][:].bitcast(I32), 0)
        nc.scalar.activation(out=warm_out[:], in_=warm[:], func=SILU)

        for r in range(4):
            nc.sync.dma_start(out=xs_sb[:].bitcast(I32)[r:P:32, :, :], in_=xs_src[r])
        load_us(us_first, 0, 256)
        make_identity(nc, ident[:])

        def load_up(j):
            nc.sync.dma_start(out=up_sb[j][:].bitcast(I32), in_=up_src[:, :, 512 * j : 512 * (j + 1)])

        def load_z(i):
            j, h = divmod(i, 2)
            nc.sync.dma_start(out=z_sb[i][:], in_=z_src[:, 2 * h : 2 * h + 2, 1024 * j : 1024 * (j + 1)])

        def load_down(j, first, end):
            nc.sync.dma_start(
                out=down_sb[j][:].bitcast(I32)[:, :, first:end], in_=down_src[:, 2 * j : 2 * j + 2, first:end]
            )

        def load_res(h):
            nc.sync.dma_start(out=res_sb[h][:], in_=res_src[:, 2 * h : 2 * h + 2, :])

        nc.sync.dma_start(out=up_sb[0][:].bitcast(I32)[:, :, 256:512], in_=up_src[:, :, 256:512])
        nc.sync.dma_start(out=z_sb[0][:, :, 512:1024], in_=z_src[:, 0:2, 512:1024])
        load_z(1)
        load_us(us_second, 256, 512)
        load_up(1)
        load_z(2)
        load_ds(0)
        load_down(0, 0, 512)
        load_z(3)
        load_down(0, 512, 1024)
        load_us(us_rest, 512, 1024)
        load_up(2)
        load_z(4)
        load_z(5)
        load_down(1, 0, 1024)
        load_up(3)
        load_z(6)
        load_ds(1)
        load_z(7)
        load_down(2, 0, 1024)
        load_res(0)
        load_down(3, 0, 1024)
        load_res(1)

        silu_t = {}
        u_ps = {}
        h_sb = {}
        t_ps = {}
        grouped = {}
        codes = {}
        scales = {}
        y_ps = {}

        def silu(i, k):
            c, m = divmod(k, 2)
            s = work.tile([P, PASS], F32, name="s", tag="s", bufs=8)
            nc.scalar.activation(
                out=s[:].rearrange("p (u w e) -> p u w e", u=2, e=2),
                in_=z_sb[i][:, m, PASS * c : PASS * (c + 1)].rearrange("p (w u e) -> p u w e", u=2, e=2),
                func=SILU,
            )
            silu_t[i, k] = s

        def first_product(i, k):
            j, h = divmod(i, 2)
            c, m = divmod(k, 2)
            mt = 2 * h + m
            bank = ("u0", "u1", "y0", "y1")[k] if i < LAG else ("u0", "u1")[k % 2]
            u = psum.tile([P, PASS], F32, name=bank, tag=bank)
            for g in range(NG):
                if j == 0:
                    us = us_first[:, g, PASS * c : PASS * (c + 1)]
                elif j == 1:
                    us = us_second[:, g, PASS * c : PASS * (c + 1)]
                else:
                    c0 = 1024 * (j - 2) + PASS * c
                    us = us_rest[:, g, c0 : c0 + PASS]
                nc.tensor.matmul_mx(
                    out=u[:],
                    lhsT=x_sb[:, g, 256 * mt : 256 * (mt + 1)].bitcast(FP4X4),
                    lhsT_scale=xs_sb[:, g, P * mt : P * (mt + 1)],
                    rhs=up_sb[j][:, g, 1024 * c : 1024 * (c + 1)].bitcast(FP4X4),
                    rhs_scale=us,
                    start=(g == 0),
                    stop=(g == NG - 1),
                )
            u_ps[i, k] = u

        def gate(i, k):
            hb = work.tile([P, PASS], BF16, name="hb", tag="hb", bufs=10, align_bytes=64)
            nc.vector.tensor_tensor(
                out=hb[:].rearrange("p (u w e) -> p u w e", u=2, e=2),
                in0=u_ps[i, k][:].rearrange("p (w u e) -> p u w e", u=2, e=2),
                in1=silu_t[i, k][:].rearrange("p (u w e) -> p u w e", u=2, e=2),
                op=MULT,
            )
            h_sb[i, k] = hb

        def transposes(i, c):
            bank = ("y2", "y3")[c] if i == 0 else ("t0", "t1")[c]
            t = psum.tile([P, 4, P], F32, name=bank, tag=bank)
            for m in range(2):
                words = h_sb[i, 2 * c + m][:].bitcast(F32)
                for u in range(2):
                    nc.tensor.transpose(t[:, 2 * m + u, :], words[:, P * u : P * (u + 1)], ident[:])
            t_ps[i, c] = t

        def copy_out(i, c, on_vector):
            if c == 0:
                grouped[i] = work.tile([P, 2, 1024], BF16, name="gr", tag="gr", bufs=2, align_bytes=64)
            dst = grouped[i][:, c, :].bitcast(F32).rearrange("p (m n u) -> p m n u", m=2, u=2)
            srcv = t_ps[i, c][:].rearrange("p (m u) n -> p m n u", u=2)
            if on_vector:
                nc.vector.tensor_copy(out=dst, in_=srcv)
            else:
                nc.scalar.copy(out=dst, in_=srcv)

        def new_codes(i):
            codes[i] = work.tile([P, 2, 256], U32, name="cd", tag="cd", bufs=STEPS, align_bytes=64)
            scales[i] = work.tile([P, 2, 256], U8, name="sc", tag="sc", bufs=STEPS, align_bytes=64)

        def quantise(i):
            new_codes(i)
            nc.vector.quantize_mx(
                out=codes[i][:].rearrange("p c n -> p (c n)").bitcast(FP8X4),
                scales=scales[i][:].rearrange("p c n -> p (c n)"),
                in_=grouped[i][:].rearrange("p c n -> p (c n)"),
            )

        def second_product(i, a, bank, col, width):
            j, h = divmod(i, 2)
            m, nh = divmod(a, 2)
            if j == 0:
                y_ps[h, a, col] = psum.tile([P, width], F32, name=bank, tag=bank)
            first = 512 * nh + col
            for c in range(2):
                g = 2 * j + c
                nc.tensor.matmul_mx(
                    out=y_ps[h, a, col][:],
                    lhsT=codes[i][:, c, P * m : P * (m + 1)].bitcast(FP8X4),
                    lhsT_scale=scales[i][:, c, P * m : P * (m + 1)],
                    rhs=down_sb[j][:, c, first : first + width].bitcast(FP8X4),
                    rhs_scale=ds_sb[g // 4][4 * (g % 4) : P, first : first + width],
                    start=(g == 0),
                    stop=(g == 2 * PAIRS - 1),
                )

        def finish(h, a, col, width):
            m, nh = divmod(a, 2)
            mt = 2 * h + m
            o = work.tile([P, 512], F32, name="o", tag="o", bufs=8)
            cols = slice(512 * nh + col, 512 * nh + col + width)
            nc.vector.tensor_tensor(out=o[:, 0:width], in0=y_ps[h, a, col][:], in1=res_sb[h][:, m, cols], op=ADD)
            nc.sync.dma_start(out=out[P * mt : P * (mt + 1), cols], in_=o[:, 0:width])

        for k in range(4):
            silu(0, k)
        for i in range(STEPS):
            for k in range(4):
                first_product(i, k)
                if i >= LAG and k % 2 == 1:
                    j, n = divmod(2 * (i - LAG) + k // 2, 4)
                    second_product(2 * j, ORDER[n], "y%d" % n, 0, 512)
                gate(i, k)
                if k == 0:
                    if i >= 1:
                        transposes(i - 1, 0)
                        transposes(i - 1, 1)
                        copy_out(i - 1, 0, False)
                        copy_out(i - 1, 1, i - 1 in (0, 2))
                    if i + 1 < STEPS:
                        for kk in range(4):
                            silu(i + 1, kk)
                if k == 1 and i >= 1:
                    quantise(i - 1)
        last = STEPS - 1
        for n in range(4):
            second_product(6, ORDER[n], "y%d" % n, 0, 512)
            finish(0, ORDER[n], 0, 512)
            if n == 0:
                transposes(last, 0)
                copy_out(last, 0, False)
                transposes(last, 1)
                copy_out(last, 1, True)
            if n == 1:
                quantise(last)
        for a in range(4):
            for col in (0,) if a < 3 else (0, 256):
                for i in range(1, STEPS, 2):
                    second_product(i, a, ("u0", "u1", "t0", "t1", "y0")[a + col // 256], col, 512 if a < 3 else 256)
                finish(1, a, col, 512 if a < 3 else 256)
